import numpy as np
import ml_dtypes


def mxq(x, axis, fmt="e4m3"):
    dtype, down = {"e4m3": (ml_dtypes.float8_e4m3fn, 7), "e5m2": (ml_dtypes.float8_e5m2, 14)}[fmt]
    v = np.moveaxis(np.asarray(x, np.float32).astype(ml_dtypes.bfloat16).astype(np.float64), axis, -1)
    blocks = v.reshape(v.shape[:-1] + (-1, 32))
    amax = np.abs(blocks).max(-1, keepdims=True)
    byte = np.maximum(np.where(amax > 0, np.frexp(amax)[1] - 1 + 127, 0) - down, 1)
    scale = np.exp2(byte - 127.0)
    codes = (blocks / scale).astype(np.float32).astype(dtype).astype(np.float64)
    return np.moveaxis((codes * scale).reshape(v.shape), -1, axis)


WIDE = False


def mx_kscale(k):
    if not WIDE:
        return np.ones(k)
    levels = np.array([10, -10, 5, -5, 0])
    if k % 512:
        return np.exp2(np.random.permutation(np.resize(levels, k // 32))).repeat(32)
    a = np.empty((k // 512, 16))
    for p in range(k // 512):
        a[p, :8] = np.random.permutation(np.resize(levels, 8))
        for g in range(8):
            far = levels[np.abs(levels - a[p, g]) >= 10]
            a[p, g + 8] = far[np.random.randint(len(far))]
    return np.exp2(a.ravel()).repeat(32)


def f64(x):
    return np.asarray(x).astype(np.float64)


def striped(idx):
    return np.tile(idx.reshape(-1, 16).T, (8, 1)).astype(np.uint16)


def unstriped(offs):
    return offs[:16].T.reshape(-1).astype(np.int64)


def pack_weight(w):
    k, n = w.shape
    w = f64(np.asarray(w, np.float32).astype(ml_dtypes.bfloat16)).reshape(k // 32, 32, n)
    amax = np.abs(w).max(1)
    byte = np.clip(np.where(amax > 0, np.frexp(amax)[1] - 1 + 127 - 7, 1), 1, 254)
    scaled = (w * np.exp2(127.0 - byte)[:, None, :]).reshape(k, n).astype(np.float32)
    words = np.ascontiguousarray(scaled.reshape(k // 512, 128, 4, n).transpose(0, 1, 3, 2)).astype(ml_dtypes.float8_e4m3fn).view(np.uint8)
    return words, np.ascontiguousarray(byte.astype(np.uint8).reshape(k // 512, 16, n))


def unpack_weight(words, scales):
    g, p, n, _ = words.shape
    vals = np.ascontiguousarray(words).view(ml_dtypes.float8_e4m3fn).astype(np.float64) * np.repeat(np.exp2(scales.astype(np.float64) - 127.0), 8, axis=1)[..., None]
    return vals.transpose(0, 1, 3, 2).reshape(g * 512, n)


K, T, S, D, N, H = 1024, 2048, 1024, 4, 128, 512


def setup_inputs():
    n = np.random.standard_normal
    s = mx_kscale(K)[:, None]
    u = mx_kscale(H)
    packed_xT = pack_weight(n((K, T)) * s)
    return {
        "x_words": packed_xT[0],
        "x_scales": packed_xT[1],
        "w1": (n((K, H)) / np.sqrt(K) / s).astype(np.float32),
        "bel": (np.random.uniform(0.1, 1.0, (H, S))).astype(np.float32),
        "unit": (np.random.uniform(0.6, 1.4, (H, 1)) * u[:, None]).astype(np.float32),
        "w2": (n((H, N)) / np.sqrt(H) / u[:, None]).astype(np.float32),
        "offs": striped(np.random.permutation(T)[:S]),
        "mv1": striped(np.random.permutation(S)),
        "mv2": striped(np.random.permutation(S)),
    }


def reference(x_words, x_scales, w1, bel, unit, w2, offs, mv1, mv2):
    pred = 0.5 * f64(bel) + 0.3 * f64(bel)[:, unstriped(mv1)] + 0.2 * f64(bel)[:, unstriped(mv2)]
    xq = unpack_weight(x_words, x_scales)[:, unstriped(offs)]
    y = mxq(f64(w1), 0, "e4m3").T @ xq
    lik = np.exp(1.2 * np.tanh(y))
    post = pred * lik
    tile = post.reshape(len(post), -1, D).sum(axis=2)
    nrm = post / (np.repeat(tile, D, axis=1) + 0.2)
    ent = -1.0 * (nrm * np.log(nrm))
    hid = f64(unit) * (nrm - (0.5 * ent))
    return mxq(f64(w2), 0, "e4m3").T @ mxq(hid, 0, "e4m3")

@@ -1,0 +1,378 @@
+import math
+from contextlib import ExitStack
+
+import concourse.mybir as mybir
+from concourse.masks import make_identity
+
+K, T, S, D, N, H = 1024, 2048, 1024, 4, 128, 512
+FLOPS = 2 * K * H * S + 2 * H * N * S
+
+F32 = mybir.dt.float32
+BF16 = mybir.dt.bfloat16
+I32 = mybir.dt.int32
+U32 = mybir.dt.uint32
+U16 = mybir.dt.uint16
+U8 = mybir.dt.uint8
+FP8X4 = mybir.dt.float8_e4m3fn_x4
+ALU = mybir.AluOpType
+ACT = mybir.ActivationFunctionType
+
+P = 128
+PACK = 4
+PASSES = K // (P * PACK)
+HALF = 512
+HALVES = S // HALF
+BLOCKS = HALF // P
+QUARTER = 256
+GROUPS = S // D
+LATE_AFTER = (1, 3)
+PIECES = ((0, 256), (256, 512), (512, 768), (768, 896), (896, 1024))
+TREE_ON_VECTOR = (3,)
+CAST_ON_GPSIMD = (0,)
+VECTOR_GATHERS = ((0, 0), (1, 0))
+RESCALED = sorted(set(t for t, h in VECTOR_GATHERS))
+
+
+def tile_picked_yhistf_ent_p_kernel(
+    tc, x_words, x_scales, w1, bel, unit, w2, offs, mv1, mv2, out
+):
+    nc = tc.nc
+    with ExitStack() as ctx:
+        keep = ctx.enter_context(tc.tile_pool(name="keep", bufs=1))
+        ring = ctx.enter_context(tc.tile_pool(name="ring", bufs=2))
+        psum = ctx.enter_context(tc.psum_pool(name="psum", bufs=2))
+
+        offs_t = keep.tile([P, S // 16], U16, name="offs_t")
+        mv1_t = keep.tile([P, S // 16], U16, name="mv1_t")
+        mv2_t = keep.tile([P, S // 16], U16, name="mv2_t")
+        bel_t = [keep.tile([P, S], F32, name=f"bel{t}") for t in range(PACK)]
+        xw = [keep.tile([P, T], I32, name=f"xw{g}") for g in range(PASSES)]
+        xs = keep.tile([P, T], U8, name="xs")
+        w1_raw = [keep.tile([P, PACK, H], F32, name=f"w1_raw{g}") for g in range(PASSES)]
+        w2_raw = keep.tile([P, PACK, N], F32, name="w2_raw")
+        unit_t = keep.tile([P, PACK], F32, name="unit_t")
+        ident = keep.tile([P, P], F32, name="ident")
+
+        make_identity(nc, ident[:])
+        nc.gpsimd.memset(xs[:].bitcast(I32), 0)
+
+        bel_rows = bel.rearrange("(p t) j -> t p j", t=PACK)
+
+        def load_words(g):
+            nc.sync.dma_start(out=xw[g][:], in_=x_words[g].rearrange("p c r -> p (c r)").bitcast(I32))
+
+        def load_w1(g):
+            rows = w1[g * P * PACK : (g + 1) * P * PACK, :]
+            nc.sync.dma_start(out=w1_raw[g][:], in_=rows.rearrange("(p j) c -> p j c", j=PACK))
+
+        def load_scales():
+            for q in range(4):
+                nc.sync.dma_start(
+                    out=xs[32 * q : 32 * q + 4 * PASSES, :].bitcast(I32),
+                    in_=x_scales[:, 4 * q : 4 * q + 4, :].bitcast(I32),
+                )
+
+        nc.sync.dma_start(out=bel_t[0][:], in_=bel_rows[0])
+        nc.sync.dma_start(mv1_t[:], mv1)
+        nc.sync.dma_start(mv2_t[:], mv2)
+        nc.sync.dma_start(out=bel_t[1][:], in_=bel_rows[1])
+        load_words(0)
+        nc.sync.dma_start(offs_t[:], offs)
+        load_scales()
+        nc.sync.dma_start(out=bel_t[2][:], in_=bel_rows[2])
+        load_w1(0)
+        load_w1(1)
+        load_words(1)
+        nc.sync.dma_start(out=bel_t[3][:], in_=bel_rows[3])
+        nc.sync.dma_start(out=unit_t[:], in_=unit.rearrange("(p t) o -> p (t o)", t=PACK))
+        nc.sync.dma_start(out=w2_raw[:], in_=w2.rearrange("(p j) m -> p j m", j=PACK))
+
+        def cols(h):
+            return slice(h * HALF // 16, (h + 1) * HALF // 16)
+
+        gw = {}
+        gs = {}
+
+        def gather_words(g, h):
+            gw[g, h] = keep.tile([P, HALF], U32, name=f"gw{g}{h}", align_bytes=64)
+            nc.vector.tensor_copy(gw[g, h][:], xw[g][:].bitcast(U32).indirect(offs_t[:, cols(h)]))
+
+        def gather_scales(h):
+            gs[h] = keep.tile([P, HALF], U8, name=f"gs{h}", align_bytes=64)
+            nc.vector.tensor_copy(gs[h][:], xs[:].indirect(offs_t[:, cols(h)]))
+
+        w1_q = [keep.tile([P, H], U32, name=f"w1_q{g}", align_bytes=64) for g in range(PASSES)]
+        w1_s = [keep.tile([P, H], U8, name=f"w1_s{g}", align_bytes=64) for g in range(PASSES)]
+        w1_b = [keep.tile([P, H * PACK], BF16, name=f"w1_b{g}", align_bytes=64) for g in range(PASSES)]
+
+        def cast_w1(g):
+            if g in CAST_ON_GPSIMD:
+                nc.gpsimd.tensor_scalar(
+                    w1_b[g][:].rearrange("p (t m j) -> p t m j", t=PACK, j=PACK),
+                    w1_raw[g][:].rearrange("p j (m t) -> p t m j", t=PACK),
+                    1.0,
+                    0.0,
+                    ALU.mult,
+                    ALU.add,
+                )
+                return
+            nc.vector.tensor_copy(
+                out=w1_b[g][:].rearrange("p (t m j) -> p m j t", t=PACK, j=PACK),
+                in_=w1_raw[g][:].rearrange("p j (m t) -> p m j t", t=PACK),
+            )
+
+        def quantize_w1(g):
+            nc.vector.quantize_mx(out=w1_q[g][:].bitcast(FP8X4), scales=w1_s[g][:], in_=w1_b[g][:])
+
+        moved = {}
+        lik = {}
+
+        def lead_weight(t):
+            return 0.3 if t in RESCALED else 0.5
+
+        stay = {t: bel_t[t] for t in range(PACK)}
+
+        def rescale(t):
+            stay[t] = keep.tile([P, S], F32, name=f"stay{t}")
+            nc.gpsimd.tensor_scalar(stay[t][:], bel_t[t][:], 0.5 / 0.3, 0.0, ALU.mult, ALU.add)
+
+        def gather_beliefs(t, h):
+            for name, lst, weight in (("a", mv1_t, 0.3), ("b", mv2_t, 0.2)):
+                if t == PACK - 1:
+                    moved[name, t, h] = lik[LATE_AFTER[h] + (name == "b")]
+                else:
+                    moved[name, t, h] = keep.tile([P, HALF], F32, name=f"moved_{name}{t}{h}")
+                looked_up = bel_t[t][:].indirect(lst[:, cols(h)])
+                if name == "a" and (t, h) in VECTOR_GATHERS:
+                    nc.vector.tensor_copy(moved[name, t, h][:], looked_up)
+                else:
+                    nc.scalar.activation(moved[name, t, h][:], looked_up, ACT.Copy, scale=weight / lead_weight(t))
+
+        logs = keep.tile([P, PACK * S], F32, name="logs")
+        scaled = keep.tile([P, PACK * S], F32, name="scaled")
+        units = [(2 * a + b, h) for a in range(2) for h in range(HALVES) for b in range(2)]
+        scratch = logs[:].rearrange("p (r n c) -> p n r c", r=len(units), n=len(units))
+
+        pred = {}
+        post = {}
+        sums = {}
+
+        def likelihood(n):
+            t, h = units[n]
+            y = psum.tile([P, HALF], F32, name="y")
+            for b in range(BLOCKS):
+                blk = slice(b * P, (b + 1) * P)
+                for g in range(PASSES):
+                    nc.tensor.matmul_mx(
+                        out=y[:, blk],
+                        lhsT=gw[g, h][:, blk].bitcast(FP8X4),
+                        lhsT_scale=gs[h][4 * g :, blk],
+                        rhs=w1_q[g][:, t * P : (t + 1) * P].bitcast(FP8X4),
+                        rhs_scale=w1_s[g][:, t * P : (t + 1) * P],
+                        start=(g == 0),
+                        stop=(g == PASSES - 1),
+                    )
+            nc.scalar.activation(scratch[:, n], y[:].rearrange("p (r c) -> p r c", r=len(units)), ACT.Tanh)
+            lik[n] = keep.tile([P, HALF], F32, name=f"lik{n}")
+            nc.scalar.activation(
+                lik[n][:].rearrange("p (r c) -> p r c", r=len(units)), scratch[:, n], ACT.Exp, scale=1.2
+            )
+
+        def prediction(n):
+            t, h = units[n]
+            pred[n] = psum.tile([P, HALF], F32, name="work", bufs=6)
+            for b in range(BLOCKS):
+                blk = slice(b * P, (b + 1) * P)
+                terms = (
+                    stay[t][:, h * HALF + b * P : h * HALF + (b + 1) * P],
+                    moved["a", t, h][:, blk],
+                    moved["b", t, h][:, blk],
+                )
+                for i, term in enumerate(terms):
+                    nc.tensor.matmul(
+                        pred[n][:, blk], term, ident[:], start=(i == 0), stop=(i == len(terms) - 1), is_transpose=True
+                    )
+
+        def posterior(n):
+            t, h = units[n]
+            turned = ring.tile([P, HALF], F32, name="turned")
+            nc.vector.tensor_tensor(turned[:], pred[n][:], lik[n][:], ALU.mult)
+            post[n] = pred[n]
+            for b in range(BLOCKS):
+                blk = slice(b * P, (b + 1) * P)
+                nc.tensor.transpose(post[n][:, blk], turned[:, blk], ident[:])
+
+        def tile_sums(n):
+            t, h = units[n]
+            if n % 2 == 0:
+                sums[n // 2] = ring.tile([P, GROUPS], F32, name="sums")
+            nc.vector.tensor_reduce(
+                sums[n // 2][:, n % 2 * P : (n % 2 + 1) * P],
+                post[n][:].rearrange("p (v d) -> p v d", d=D),
+                mybir.AxisListType.X,
+                ALU.add,
+            )
+
+        inverse = {}
+
+        def halves(ap):
+            return ap.rearrange("p (a n) -> p a n", a=2)
+
+        def reciprocals(t):
+            mul = nc.vector if t in TREE_ON_VECTOR else nc.gpsimd
+            den = ring.tile([P, GROUPS], F32, name="den")
+            mul.tensor_scalar(den[:], sums[t][:], 1.0, 0.2 / lead_weight(units[2 * t][0]), ALU.mult, ALU.add)
+            pair = ring.tile([P, GROUPS // 2], F32, name="pair")
+            mul.tensor_tensor(pair[:], den[:, : GROUPS // 2], den[:, GROUPS // 2 :], ALU.mult)
+            quad = ring.tile([P, GROUPS // 4], F32, name="quad")
+            mul.tensor_tensor(quad[:], pair[:, : GROUPS // 4], pair[:, GROUPS // 4 :], ALU.mult)
+            quad_inv = ring.tile([P, GROUPS // 4], F32, name="quad_inv")
+            nc.vector.reciprocal(quad_inv[:], quad[:])
+            pair_inv = ring.tile([P, GROUPS // 2], F32, name="pair_inv")
+            mul.tensor_tensor(
+                halves(pair_inv[:]),
+                halves(pair[:])[:, ::-1, :],
+                quad_inv[:].unsqueeze(1).to_broadcast([P, 2, GROUPS // 4]),
+                ALU.mult,
+            )
+            inverse[t] = ring.tile([P, GROUPS], F32, name="inverse")
+            mul.tensor_tensor(
+                halves(inverse[t][:]),
+                halves(den[:])[:, ::-1, :],
+                pair_inv[:].unsqueeze(1).to_broadcast([P, 2, GROUPS // 2]),
+                ALU.mult,
+            )
+
+        half_unit = keep.tile([P, PACK], F32, name="half_unit")
+        is_zero = keep.tile([P, PACK], F32, name="is_zero")
+        safe = keep.tile([P, PACK], F32, name="safe")
+        safe_inv = keep.tile([P, PACK], F32, name="safe_inv")
+        log_scale = keep.tile([P, PACK], F32, name="log_scale")
+
+        def unit_factors():
+            nc.gpsimd.tensor_scalar(half_unit[:], unit_t[:], 0.5, 0.0, ALU.mult, ALU.add)
+            nc.gpsimd.tensor_single_scalar(is_zero[:], unit_t[:], 0.0, ALU.is_equal)
+            nc.gpsimd.tensor_tensor(safe[:], unit_t[:], is_zero[:], ALU.add)
+            nc.vector.reciprocal(safe_inv[:], safe[:])
+            nc.gpsimd.tensor_scalar(log_scale[:], safe_inv[:], 2.0 * math.exp(2.0), 0.0, ALU.mult, ALU.add)
+
+        def region(tile, n):
+            t, h = units[n]
+            return tile[:, t * S + h * HALF : t * S + (h + 1) * HALF]
+
+        def normalise(n):
+            t, h = units[n]
+            nc.vector.scalar_tensor_tensor(
+                region(scaled, n).rearrange("p (v d) -> p v d", d=D),
+                post[n][:].rearrange("p (v d) -> p v d", d=D),
+                half_unit[:, t : t + 1],
+                inverse[n // 2][:, n % 2 * P : (n % 2 + 1) * P].unsqueeze(2).to_broadcast([P, P, D]),
+                ALU.mult,
+                ALU.mult,
+            )
+
+        def logarithm(n):
+            t, h = units[n]
+            nc.scalar.activation(
+                region(logs, n), region(scaled, n), ACT.Ln, scale=log_scale[:, t : t + 1], bias=is_zero[:, t : t + 1]
+            )
+
+        w2_b = keep.tile([P, N * PACK], BF16, name="w2_b", align_bytes=64)
+        w2_q = keep.tile([P, N], U32, name="w2_q", align_bytes=64)
+        w2_s = keep.tile([P, N], U8, name="w2_s", align_bytes=64)
+
+        def quantize_w2():
+            nc.gpsimd.tensor_scalar(
+                w2_b[:].rearrange("p (m j) -> p m j", j=PACK),
+                w2_raw[:].rearrange("p j m -> p m j"),
+                1.0,
+                0.0,
+                ALU.mult,
+                ALU.add,
+            )
+            nc.vector.quantize_mx(out=w2_q[:].bitcast(FP8X4), scales=w2_s[:], in_=w2_b[:])
+
+        hid = {}
+
+        def hidden(q):
+            c0, c1 = PIECES[q]
+
+            def walk(tile):
+                planes = tile[:].rearrange("p (t j) -> p t j", t=PACK)[:, :, c0:c1]
+                return planes.rearrange("p t (c i) -> p c t i", i=4)
+
+            hid[q] = ring.tile([P, (c1 - c0) * PACK], BF16, name="hid", align_bytes=64, bufs=3)
+            nc.vector.tensor_tensor(
+                hid[q][:].rearrange("p (c i t) -> p c t i", i=4, t=PACK), walk(scaled), walk(logs), ALU.mult
+            )
+
+        def poses(q):
+            c0, c1 = PIECES[q]
+            width = c1 - c0
+            hid_q = ring.tile([P, width], U32, name="hid_q", align_bytes=64)
+            hid_s = ring.tile([P, width], U8, name="hid_s", align_bytes=64)
+            nc.vector.quantize_mx(out=hid_q[:].bitcast(FP8X4), scales=hid_s[:], in_=hid[q][:])
+            acc = psum.tile([P, HALF], F32, name="y")
+            nc.tensor.matmul_mx(
+                out=acc[:, :width],
+                lhsT=w2_q[:].bitcast(FP8X4),
+                lhsT_scale=w2_s[:],
+                rhs=hid_q[:].bitcast(FP8X4),
+                rhs_scale=hid_s[:],
+                start=True,
+                stop=True,
+            )
+            result = ring.tile([P, width], F32, name="result", bufs=len(PIECES))
+            nc.scalar.copy(result[:], acc[:, :width])
+            nc.sync.dma_start(out=out[:, c0:c1], in_=result[:])
+
+        for t in RESCALED:
+            rescale(t)
+        for t in range(PACK - 1):
+            for h in range(HALVES):
+                gather_beliefs(t, h)
+        gather_words(0, 0)
+        cast_w1(0)
+        gather_scales(0)
+        quantize_w1(0)
+        cast_w1(1)
+        gather_words(0, 1)
+        quantize_w1(1)
+        gather_words(1, 0)
+        for n in (0, 1, 2, 3, 4):
+            prediction(n)
+        for step in range(len(units) + 3):
+            if step < len(units):
+                likelihood(step)
+            if step == 0:
+                gather_words(1, 1)
+                gather_scales(1)
+            if step == 2:
+                unit_factors()
+            if step == 4:
+                quantize_w2()
+            if 1 <= step <= len(units):
+                posterior(step - 1)
+            if step == LATE_AFTER[0] + 2:
+                gather_beliefs(PACK - 1, 0)
+                prediction(5)
+            if step == LATE_AFTER[1] + 2:
+                gather_beliefs(PACK - 1, 1)
+            if 2 <= step <= len(units) + 1:
+                tile_sums(step - 2)
+                if step % 2 == 1:
+                    reciprocals((step - 2) // 2)
+            if step >= 4 and step % 2 == 0:
+                normalise(step - 4)
+                normalise(step - 3)
+            if step == 4:
+                prediction(6)
+            if step == 6:
+                prediction(7)
+        for n in sorted(range(len(units)), key=lambda n: units[n][1]):
+            logarithm(n)
+        for q in range(len(PIECES) + 1):
+            if q < len(PIECES):
+                hidden(q)
+            if q >= 1:
+                poses(q - 1)

@@ -23,14 +23,16 @@ PASSES = K // (P * PACK)
 HALF = 512
 HALVES = S // HALF
 BLOCKS = HALF // P
-QUARTER = 256
-GROUPS = S // D
-LATE_AFTER = (1, 3)
-PIECES = ((0, 256), (256, 512), (512, 768), (768, 896), (896, 1024))
-TREE_ON_VECTOR = (3,)
-CAST_ON_GPSIMD = (0,)
-VECTOR_GATHERS = ((0, 0), (1, 0))
+GROUPS = 2 * HALF // D
+UNITS = [(t, h) for h in range(HALVES) for t in range(PACK)]
+WORK_BANKS = 6
+CAST_ON_GPSIMD = (0, 1)
+VECTOR_GATHERS = ((0, 0), (1, 0), (0, 1), (1, 1))
 RESCALED = sorted(set(t for t, h in VECTOR_GATHERS))
+TREE_ON_VECTOR = (3,)
+LATE_AFTER = {}
+PIECES = ((0, 256), (256, 512), (512, 640), (640, 768), (768, 896), (896, 1024))
+WEAVE_ON_SCALAR = (0, 1, 2, 4)
 
 
 def tile_picked_yhistf_ent_p_kernel(
@@ -46,20 +48,23 @@ def tile_picked_yhistf_ent_p_kernel(
         mv1_t = keep.tile([P, S // 16], U16, name="mv1_t")
         mv2_t = keep.tile([P, S // 16], U16, name="mv2_t")
         bel_t = [keep.tile([P, S], F32, name=f"bel{t}") for t in range(PACK)]
-        xw = [keep.tile([P, T], I32, name=f"xw{g}") for g in range(PASSES)]
+        xw = keep.tile([P, PASSES * T], I32, name="xw")
         xs = keep.tile([P, T], U8, name="xs")
         w1_raw = [keep.tile([P, PACK, H], F32, name=f"w1_raw{g}") for g in range(PASSES)]
         w2_raw = keep.tile([P, PACK, N], F32, name="w2_raw")
         unit_t = keep.tile([P, PACK], F32, name="unit_t")
         ident = keep.tile([P, P], F32, name="ident")
 
-        make_identity(nc, ident[:])
         nc.gpsimd.memset(xs[:].bitcast(I32), 0)
+        make_identity(nc, ident[:])
 
         bel_rows = bel.rearrange("(p t) j -> t p j", t=PACK)
 
+        def load_beliefs(t):
+            nc.sync.dma_start(out=bel_t[t][:], in_=bel_rows[t])
+
         def load_words(g):
-            nc.sync.dma_start(out=xw[g][:], in_=x_words[g].rearrange("p c r -> p (c r)").bitcast(I32))
+            nc.sync.dma_start(out=xw[:, g * T : (g + 1) * T], in_=x_words[g].rearrange("p c r -> p (c r)").bitcast(I32))
 
         def load_w1(g):
             rows = w1[g * P * PACK : (g + 1) * P * PACK, :]
@@ -72,18 +77,18 @@ def tile_picked_yhistf_ent_p_kernel(
                     in_=x_scales[:, 4 * q : 4 * q + 4, :].bitcast(I32),
                 )
 
-        nc.sync.dma_start(out=bel_t[0][:], in_=bel_rows[0])
+        load_beliefs(0)
         nc.sync.dma_start(mv1_t[:], mv1)
         nc.sync.dma_start(mv2_t[:], mv2)
-        nc.sync.dma_start(out=bel_t[1][:], in_=bel_rows[1])
-        load_words(0)
-        nc.sync.dma_start(offs_t[:], offs)
-        load_scales()
-        nc.sync.dma_start(out=bel_t[2][:], in_=bel_rows[2])
+        load_beliefs(1)
+        load_beliefs(2)
         load_w1(0)
         load_w1(1)
+        nc.sync.dma_start(offs_t[:], offs)
+        load_scales()
+        load_beliefs(3)
+        load_words(0)
         load_words(1)
-        nc.sync.dma_start(out=bel_t[3][:], in_=bel_rows[3])
         nc.sync.dma_start(out=unit_t[:], in_=unit.rearrange("(p t) o -> p (t o)", t=PACK))
         nc.sync.dma_start(out=w2_raw[:], in_=w2.rearrange("(p j) m -> p j m", j=PACK))
 
@@ -95,7 +100,8 @@ def tile_picked_yhistf_ent_p_kernel(
 
         def gather_words(g, h):
             gw[g, h] = keep.tile([P, HALF], U32, name=f"gw{g}{h}", align_bytes=64)
-            nc.vector.tensor_copy(gw[g, h][:], xw[g][:].bitcast(U32).indirect(offs_t[:, cols(h)]))
+            end = (g + 1) * T if h == 0 else PASSES * T
+            nc.vector.tensor_copy(gw[g, h][:], xw[:, g * T : end].bitcast(U32).indirect(offs_t[:, cols(h)]))
 
         def gather_scales(h):
             gs[h] = keep.tile([P, HALF], U8, name=f"gs{h}", align_bytes=64)
@@ -115,11 +121,11 @@ def tile_picked_yhistf_ent_p_kernel(
                     ALU.mult,
                     ALU.add,
                 )
-                return
-            nc.vector.tensor_copy(
-                out=w1_b[g][:].rearrange("p (t m j) -> p m j t", t=PACK, j=PACK),
-                in_=w1_raw[g][:].rearrange("p j (m t) -> p m j t", t=PACK),
-            )
+            else:
+                nc.vector.tensor_copy(
+                    out=w1_b[g][:].rearrange("p (t m j) -> p m j t", t=PACK, j=PACK),
+                    in_=w1_raw[g][:].rearrange("p j (m t) -> p m j t", t=PACK),
+                )
 
         def quantize_w1(g):
             nc.vector.quantize_mx(out=w1_q[g][:].bitcast(FP8X4), scales=w1_s[g][:], in_=w1_b[g][:])
@@ -137,28 +143,26 @@ def tile_picked_yhistf_ent_p_kernel(
             nc.gpsimd.tensor_scalar(stay[t][:], bel_t[t][:], 0.5 / 0.3, 0.0, ALU.mult, ALU.add)
 
         def gather_beliefs(t, h):
-            for name, lst, weight in (("a", mv1_t, 0.3), ("b", mv2_t, 0.2)):
-                if t == PACK - 1:
-                    moved[name, t, h] = lik[LATE_AFTER[h] + (name == "b")]
+            for which, lst, weight in ((0, mv1_t, 0.3), (1, mv2_t, 0.2)):
+                if (t, h, which) in LATE_AFTER:
+                    moved[which, t, h] = lik[LATE_AFTER[t, h, which]]
                 else:
-                    moved[name, t, h] = keep.tile([P, HALF], F32, name=f"moved_{name}{t}{h}")
+                    moved[which, t, h] = keep.tile([P, HALF], F32, name=f"moved_{which}{t}{h}")
                 looked_up = bel_t[t][:].indirect(lst[:, cols(h)])
-                if name == "a" and (t, h) in VECTOR_GATHERS:
-                    nc.vector.tensor_copy(moved[name, t, h][:], looked_up)
+                if which == 0 and (t, h) in VECTOR_GATHERS:
+                    nc.vector.tensor_copy(moved[which, t, h][:], looked_up)
                 else:
-                    nc.scalar.activation(moved[name, t, h][:], looked_up, ACT.Copy, scale=weight / lead_weight(t))
+                    nc.scalar.activation(moved[which, t, h][:], looked_up, ACT.Copy, scale=weight / lead_weight(t))
 
         logs = keep.tile([P, PACK * S], F32, name="logs")
-        scaled = keep.tile([P, PACK * S], F32, name="scaled")
-        units = [(2 * a + b, h) for a in range(2) for h in range(HALVES) for b in range(2)]
-        scratch = logs[:].rearrange("p (r n c) -> p n r c", r=len(units), n=len(units))
+        normed = keep.tile([P, PACK * S], F32, name="normed")
+        scratch = logs[:].rearrange("p (r n c) -> p n r c", r=len(UNITS), n=len(UNITS))
 
-        pred = {}
-        post = {}
+        work = {}
         sums = {}
 
         def likelihood(n):
-            t, h = units[n]
+            t, h = UNITS[n]
             y = psum.tile([P, HALF], F32, name="y")
             for b in range(BLOCKS):
                 blk = slice(b * P, (b + 1) * P)
@@ -172,43 +176,40 @@ def tile_picked_yhistf_ent_p_kernel(
                         start=(g == 0),
                         stop=(g == PASSES - 1),
                     )
-            nc.scalar.activation(scratch[:, n], y[:].rearrange("p (r c) -> p r c", r=len(units)), ACT.Tanh)
+            nc.scalar.activation(scratch[:, n], y[:].rearrange("p (r c) -> p r c", r=len(UNITS)), ACT.Tanh)
             lik[n] = keep.tile([P, HALF], F32, name=f"lik{n}")
             nc.scalar.activation(
-                lik[n][:].rearrange("p (r c) -> p r c", r=len(units)), scratch[:, n], ACT.Exp, scale=1.2
+                lik[n][:].rearrange("p (r c) -> p r c", r=len(UNITS)), scratch[:, n], ACT.Exp, scale=1.2
             )
 
         def prediction(n):
-            t, h = units[n]
-            pred[n] = psum.tile([P, HALF], F32, name="work", bufs=6)
+            t, h = UNITS[n]
+            work[n] = psum.tile([P, HALF], F32, name="work", bufs=WORK_BANKS)
             for b in range(BLOCKS):
                 blk = slice(b * P, (b + 1) * P)
                 terms = (
                     stay[t][:, h * HALF + b * P : h * HALF + (b + 1) * P],
-                    moved["a", t, h][:, blk],
-                    moved["b", t, h][:, blk],
+                    moved[0, t, h][:, blk],
+                    moved[1, t, h][:, blk],
                 )
                 for i, term in enumerate(terms):
                     nc.tensor.matmul(
-                        pred[n][:, blk], term, ident[:], start=(i == 0), stop=(i == len(terms) - 1), is_transpose=True
+                        work[n][:, blk], term, ident[:], start=(i == 0), stop=(i == len(terms) - 1), is_transpose=True
                     )
 
         def posterior(n):
-            t, h = units[n]
             turned = ring.tile([P, HALF], F32, name="turned")
-            nc.vector.tensor_tensor(turned[:], pred[n][:], lik[n][:], ALU.mult)
-            post[n] = pred[n]
+            nc.vector.tensor_tensor(turned[:], work[n][:], lik[n][:], ALU.mult)
             for b in range(BLOCKS):
                 blk = slice(b * P, (b + 1) * P)
-                nc.tensor.transpose(post[n][:, blk], turned[:, blk], ident[:])
+                nc.tensor.transpose(work[n][:, blk], turned[:, blk], ident[:])
 
         def tile_sums(n):
-            t, h = units[n]
             if n % 2 == 0:
                 sums[n // 2] = ring.tile([P, GROUPS], F32, name="sums")
             nc.vector.tensor_reduce(
                 sums[n // 2][:, n % 2 * P : (n % 2 + 1) * P],
-                post[n][:].rearrange("p (v d) -> p v d", d=D),
+                work[n][:].rearrange("p (v d) -> p v d", d=D),
                 mybir.AxisListType.X,
                 ALU.add,
             )
@@ -218,10 +219,10 @@ def tile_picked_yhistf_ent_p_kernel(
         def halves(ap):
             return ap.rearrange("p (a n) -> p a n", a=2)
 
-        def reciprocals(t):
-            mul = nc.vector if t in TREE_ON_VECTOR else nc.gpsimd
+        def reciprocals(k):
+            mul = nc.vector if k in TREE_ON_VECTOR else nc.gpsimd
             den = ring.tile([P, GROUPS], F32, name="den")
-            mul.tensor_scalar(den[:], sums[t][:], 1.0, 0.2 / lead_weight(units[2 * t][0]), ALU.mult, ALU.add)
+            mul.tensor_scalar(den[:], sums[k][:], 1.0, 0.2 / lead_weight(UNITS[2 * k][0]), ALU.mult, ALU.add)
             pair = ring.tile([P, GROUPS // 2], F32, name="pair")
             mul.tensor_tensor(pair[:], den[:, : GROUPS // 2], den[:, GROUPS // 2 :], ALU.mult)
             quad = ring.tile([P, GROUPS // 4], F32, name="quad")
@@ -235,46 +236,40 @@ def tile_picked_yhistf_ent_p_kernel(
                 quad_inv[:].unsqueeze(1).to_broadcast([P, 2, GROUPS // 4]),
                 ALU.mult,
             )
-            inverse[t] = ring.tile([P, GROUPS], F32, name="inverse")
+            inverse[k] = ring.tile([P, GROUPS], F32, name="inverse")
             mul.tensor_tensor(
-                halves(inverse[t][:]),
+                halves(inverse[k][:]),
                 halves(den[:])[:, ::-1, :],
                 pair_inv[:].unsqueeze(1).to_broadcast([P, 2, GROUPS // 2]),
                 ALU.mult,
             )
 
         half_unit = keep.tile([P, PACK], F32, name="half_unit")
-        is_zero = keep.tile([P, PACK], F32, name="is_zero")
-        safe = keep.tile([P, PACK], F32, name="safe")
-        safe_inv = keep.tile([P, PACK], F32, name="safe_inv")
-        log_scale = keep.tile([P, PACK], F32, name="log_scale")
 
         def unit_factors():
             nc.gpsimd.tensor_scalar(half_unit[:], unit_t[:], 0.5, 0.0, ALU.mult, ALU.add)
-            nc.gpsimd.tensor_single_scalar(is_zero[:], unit_t[:], 0.0, ALU.is_equal)
-            nc.gpsimd.tensor_tensor(safe[:], unit_t[:], is_zero[:], ALU.add)
-            nc.vector.reciprocal(safe_inv[:], safe[:])
-            nc.gpsimd.tensor_scalar(log_scale[:], safe_inv[:], 2.0 * math.exp(2.0), 0.0, ALU.mult, ALU.add)
 
         def region(tile, n):
-            t, h = units[n]
+            t, h = UNITS[n]
             return tile[:, t * S + h * HALF : t * S + (h + 1) * HALF]
 
         def normalise(n):
-            t, h = units[n]
-            nc.vector.scalar_tensor_tensor(
-                region(scaled, n).rearrange("p (v d) -> p v d", d=D),
-                post[n][:].rearrange("p (v d) -> p v d", d=D),
-                half_unit[:, t : t + 1],
+            nc.vector.tensor_tensor(
+                region(normed, n).rearrange("p (v d) -> p v d", d=D),
+                work[n][:].rearrange("p (v d) -> p v d", d=D),
                 inverse[n // 2][:, n % 2 * P : (n % 2 + 1) * P].unsqueeze(2).to_broadcast([P, P, D]),
-                ALU.mult,
                 ALU.mult,
             )
 
         def logarithm(n):
-            t, h = units[n]
-            nc.scalar.activation(
-                region(logs, n), region(scaled, n), ACT.Ln, scale=log_scale[:, t : t + 1], bias=is_zero[:, t : t + 1]
+            nc.scalar.activation(region(logs, n), region(normed, n), ACT.Ln, scale=math.exp(2.0))
+
+        hid_planes = keep.tile([P, PACK * S], BF16, name="hid_planes")
+
+        def hidden(n):
+            t, h = UNITS[n]
+            nc.vector.scalar_tensor_tensor(
+                region(hid_planes, n), region(normed, n), half_unit[:, t : t + 1], region(logs, n), ALU.mult, ALU.mult
             )
 
         w2_b = keep.tile([P, N * PACK], BF16, name="w2_b", align_bytes=64)
@@ -294,23 +289,22 @@ def tile_picked_yhistf_ent_p_kernel(
 
         hid = {}
 
-        def hidden(q):
+        def weave(q):
             c0, c1 = PIECES[q]
-
-            def walk(tile):
-                planes = tile[:].rearrange("p (t j) -> p t j", t=PACK)[:, :, c0:c1]
-                return planes.rearrange("p t (c i) -> p c t i", i=4)
-
-            hid[q] = ring.tile([P, (c1 - c0) * PACK], BF16, name="hid", align_bytes=64, bufs=3)
-            nc.vector.tensor_tensor(
-                hid[q][:].rearrange("p (c i t) -> p c t i", i=4, t=PACK), walk(scaled), walk(logs), ALU.mult
-            )
+            planes = hid_planes[:].rearrange("p (t j) -> p t j", t=PACK)[:, :, c0:c1]
+            hid[q] = keep.tile([P, (c1 - c0) * PACK], BF16, name=f"hid{q}", align_bytes=64)
+            src = planes.rearrange("p t (c i) -> p c t i", i=4)
+            dst = hid[q][:].rearrange("p (c i t) -> p c t i", i=4, t=PACK)
+            if q in WEAVE_ON_SCALAR:
+                nc.scalar.copy(dst, src)
+            else:
+                nc.vector.tensor_copy(dst, src)
 
         def poses(q):
             c0, c1 = PIECES[q]
             width = c1 - c0
-            hid_q = ring.tile([P, width], U32, name="hid_q", align_bytes=64)
-            hid_s = ring.tile([P, width], U8, name="hid_s", align_bytes=64)
+            hid_q = keep.tile([P, width], U32, name=f"hid_q{q}", align_bytes=64)
+            hid_s = keep.tile([P, width], U8, name=f"hid_s{q}", align_bytes=64)
             nc.vector.quantize_mx(out=hid_q[:].bitcast(FP8X4), scales=hid_s[:], in_=hid[q][:])
             acc = psum.tile([P, HALF], F32, name="y")
             nc.tensor.matmul_mx(
@@ -322,57 +316,65 @@ def tile_picked_yhistf_ent_p_kernel(
                 start=True,
                 stop=True,
             )
-            result = ring.tile([P, width], F32, name="result", bufs=len(PIECES))
+            result = keep.tile([P, width], F32, name=f"result{q}")
             nc.scalar.copy(result[:], acc[:, :width])
             nc.sync.dma_start(out=out[:, c0:c1], in_=result[:])
 
         for t in RESCALED:
             rescale(t)
-        for t in range(PACK - 1):
-            for h in range(HALVES):
-                gather_beliefs(t, h)
-        gather_words(0, 0)
+        early = [u for u in UNITS if u + (1,) not in LATE_AFTER]
+        for t, h in sorted(early, key=lambda u: (u[0] // 2, u[1])):
+            gather_beliefs(t, h)
         cast_w1(0)
         gather_scales(0)
         quantize_w1(0)
         cast_w1(1)
-        gather_words(0, 1)
+        gather_words(0, 0)
         quantize_w1(1)
         gather_words(1, 0)
-        for n in (0, 1, 2, 3, 4):
-            prediction(n)
-        for step in range(len(units) + 3):
-            if step < len(units):
+        gather_scales(1)
+        gather_words(0, 1)
+        predicted = []
+
+        def predict_ready(done):
+            for n, (t, h) in enumerate(UNITS):
+                if n not in predicted and (1, t, h) in moved and n - WORK_BANKS < done and len(predicted) == n:
+                    prediction(n)
+                    predicted.append(n)
+
+        done = 0
+        predict_ready(done)
+        for step in range(len(UNITS) + 3):
+            if step < len(UNITS):
                 likelihood(step)
             if step == 0:
                 gather_words(1, 1)
-                gather_scales(1)
             if step == 2:
                 unit_factors()
             if step == 4:
                 quantize_w2()
-            if 1 <= step <= len(units):
+            if 1 <= step <= len(UNITS):
                 posterior(step - 1)
-            if step == LATE_AFTER[0] + 2:
-                gather_beliefs(PACK - 1, 0)
-                prediction(5)
-            if step == LATE_AFTER[1] + 2:
-                gather_beliefs(PACK - 1, 1)
-            if 2 <= step <= len(units) + 1:
+            for t, h in UNITS:
+                if LATE_AFTER.get((t, h, 1)) == step - 1:
+                    gather_beliefs(t, h)
+            if 2 <= step <= len(UNITS) + 1:
                 tile_sums(step - 2)
                 if step % 2 == 1:
                     reciprocals((step - 2) // 2)
             if step >= 4 and step % 2 == 0:
                 normalise(step - 4)
                 normalise(step - 3)
-            if step == 4:
-                prediction(6)
-            if step == 6:
-                prediction(7)
-        for n in sorted(range(len(units)), key=lambda n: units[n][1]):
+                done = step - 2
+            predict_ready(done)
+        by_half = sorted(range(len(UNITS)), key=lambda n: UNITS[n][1])
+        for n in by_half:
             logarithm(n)
-        for q in range(len(PIECES) + 1):
-            if q < len(PIECES):
-                hidden(q)
-            if q >= 1:
-                poses(q - 1)
+        for h in range(HALVES):
+            for n in by_half[h * PACK : (h + 1) * PACK]:
+                hidden(n)
+            mine = [q for q in range(len(PIECES)) if PIECES[q][0] // HALF == h]
+            for q in mine:
+                weave(q)
+            for q in mine:
+                poses(q)

@@ -24,15 +24,15 @@ HALF = 512
 HALVES = S // HALF
 BLOCKS = HALF // P
 GROUPS = 2 * HALF // D
-UNITS = [(t, h) for h in range(HALVES) for t in range(PACK)]
-WORK_BANKS = 6
-CAST_ON_GPSIMD = (0, 1)
-VECTOR_GATHERS = ((0, 0), (1, 0), (0, 1), (1, 1))
+UNITS = [(2 * a + b, h) for a in range(2) for h in range(HALVES) for b in range(2)]
+WORK_BANKS = 5
+CAST_ON_GPSIMD = ()
+VECTOR_GATHERS = ()
 RESCALED = sorted(set(t for t, h in VECTOR_GATHERS))
-TREE_ON_VECTOR = (3,)
-LATE_AFTER = {}
-PIECES = ((0, 256), (256, 512), (512, 640), (640, 768), (768, 896), (896, 1024))
-WEAVE_ON_SCALAR = (0, 1, 2, 4)
+TREE_ON_VECTOR = (0, 1, 2, 3)
+LATE_AFTER = {(3, 0, 0): 0, (3, 0, 1): 1, (2, 1, 0): 2, (2, 1, 1): 3, (3, 1, 0): 4, (3, 1, 1): 5}
+PIECES = ((0, 128), (128, 256), (256, 384), (384, 512), (512, 768), (768, 896), (896, 1024))
+WEAVE_ON_SCALAR = (0, 1)
 
 
 def tile_picked_yhistf_ent_p_kernel(
@@ -48,7 +48,7 @@ def tile_picked_yhistf_ent_p_kernel(
         mv1_t = keep.tile([P, S // 16], U16, name="mv1_t")
         mv2_t = keep.tile([P, S // 16], U16, name="mv2_t")
         bel_t = [keep.tile([P, S], F32, name=f"bel{t}") for t in range(PACK)]
-        xw = keep.tile([P, PASSES * T], I32, name="xw")
+        xw = [keep.tile([P, T], I32, name=f"xw{g}") for g in range(PASSES)]
         xs = keep.tile([P, T], U8, name="xs")
         w1_raw = [keep.tile([P, PACK, H], F32, name=f"w1_raw{g}") for g in range(PASSES)]
         w2_raw = keep.tile([P, PACK, N], F32, name="w2_raw")
@@ -64,7 +64,7 @@ def tile_picked_yhistf_ent_p_kernel(
             nc.sync.dma_start(out=bel_t[t][:], in_=bel_rows[t])
 
         def load_words(g):
-            nc.sync.dma_start(out=xw[:, g * T : (g + 1) * T], in_=x_words[g].rearrange("p c r -> p (c r)").bitcast(I32))
+            nc.sync.dma_start(out=xw[g][:], in_=x_words[g].rearrange("p c r -> p (c r)").bitcast(I32))
 
         def load_w1(g):
             rows = w1[g * P * PACK : (g + 1) * P * PACK, :]
@@ -80,15 +80,15 @@ def tile_picked_yhistf_ent_p_kernel(
         load_beliefs(0)
         nc.sync.dma_start(mv1_t[:], mv1)
         nc.sync.dma_start(mv2_t[:], mv2)
-        load_beliefs(1)
-        load_beliefs(2)
-        load_w1(0)
-        load_w1(1)
-        nc.sync.dma_start(offs_t[:], offs)
-        load_scales()
-        load_beliefs(3)
         load_words(0)
+        nc.sync.dma_start(offs_t[:], offs)
+        load_beliefs(1)
+        load_scales()
+        load_w1(0)
+        load_beliefs(2)
+        load_w1(1)
         load_words(1)
+        load_beliefs(3)
         nc.sync.dma_start(out=unit_t[:], in_=unit.rearrange("(p t) o -> p (t o)", t=PACK))
         nc.sync.dma_start(out=w2_raw[:], in_=w2.rearrange("(p j) m -> p j m", j=PACK))
 
@@ -100,8 +100,7 @@ def tile_picked_yhistf_ent_p_kernel(
 
         def gather_words(g, h):
             gw[g, h] = keep.tile([P, HALF], U32, name=f"gw{g}{h}", align_bytes=64)
-            end = (g + 1) * T if h == 0 else PASSES * T
-            nc.vector.tensor_copy(gw[g, h][:], xw[:, g * T : end].bitcast(U32).indirect(offs_t[:, cols(h)]))
+            nc.vector.tensor_copy(gw[g, h][:], xw[g][:].bitcast(U32).indirect(offs_t[:, cols(h)]))
 
         def gather_scales(h):
             gs[h] = keep.tile([P, HALF], U8, name=f"gs{h}", align_bytes=64)
@@ -158,12 +157,17 @@ def tile_picked_yhistf_ent_p_kernel(
         normed = keep.tile([P, PACK * S], F32, name="normed")
         scratch = logs[:].rearrange("p (r n c) -> p n r c", r=len(UNITS), n=len(UNITS))
 
+        banks = [psum.tile([P, HALF], F32, name=f"bank{i}", bufs=1) for i in range(8)]
+
+        def spare_bank(i):
+            return banks[WORK_BANKS + i % (8 - WORK_BANKS)]
+
         work = {}
         sums = {}
 
         def likelihood(n):
             t, h = UNITS[n]
-            y = psum.tile([P, HALF], F32, name="y")
+            y = banks[WORK_BANKS - 1] if n == 0 else spare_bank(n - 1)
             for b in range(BLOCKS):
                 blk = slice(b * P, (b + 1) * P)
                 for g in range(PASSES):
@@ -184,7 +188,7 @@ def tile_picked_yhistf_ent_p_kernel(
 
         def prediction(n):
             t, h = UNITS[n]
-            work[n] = psum.tile([P, HALF], F32, name="work", bufs=WORK_BANKS)
+            work[n] = banks[n % WORK_BANKS]
             for b in range(BLOCKS):
                 blk = slice(b * P, (b + 1) * P)
                 terms = (
@@ -246,30 +250,41 @@ def tile_picked_yhistf_ent_p_kernel(
 
         half_unit = keep.tile([P, PACK], F32, name="half_unit")
 
+        is_zero = keep.tile([P, PACK], F32, name="is_zero")
+        safe = keep.tile([P, PACK], F32, name="safe")
+        safe_inv = keep.tile([P, PACK], F32, name="safe_inv")
+        log_scale = keep.tile([P, PACK], F32, name="log_scale")
+
         def unit_factors():
-            nc.gpsimd.tensor_scalar(half_unit[:], unit_t[:], 0.5, 0.0, ALU.mult, ALU.add)
+            nc.vector.tensor_scalar_mul(half_unit[:], unit_t[:], 0.5)
+            nc.vector.tensor_single_scalar(is_zero[:], unit_t[:], 0.0, ALU.is_equal)
+            nc.vector.tensor_tensor(safe[:], unit_t[:], is_zero[:], ALU.add)
+            nc.vector.reciprocal(safe_inv[:], safe[:])
+            nc.vector.tensor_scalar_mul(log_scale[:], safe_inv[:], 2.0 * math.exp(2.0))
 
         def region(tile, n):
             t, h = UNITS[n]
             return tile[:, t * S + h * HALF : t * S + (h + 1) * HALF]
 
         def normalise(n):
-            nc.vector.tensor_tensor(
+            t = UNITS[n][0]
+            nc.vector.scalar_tensor_tensor(
                 region(normed, n).rearrange("p (v d) -> p v d", d=D),
                 work[n][:].rearrange("p (v d) -> p v d", d=D),
+                half_unit[:, t : t + 1],
                 inverse[n // 2][:, n % 2 * P : (n % 2 + 1) * P].unsqueeze(2).to_broadcast([P, P, D]),
+                ALU.mult,
                 ALU.mult,
             )
 
-        def logarithm(n):
-            nc.scalar.activation(region(logs, n), region(normed, n), ACT.Ln, scale=math.exp(2.0))
-
-        hid_planes = keep.tile([P, PACK * S], BF16, name="hid_planes")
-
-        def hidden(n):
-            t, h = UNITS[n]
-            nc.vector.scalar_tensor_tensor(
-                region(hid_planes, n), region(normed, n), half_unit[:, t : t + 1], region(logs, n), ALU.mult, ALU.mult
+        def logarithm(n, c0=0, c1=HALF):
+            t = UNITS[n][0]
+            nc.scalar.activation(
+                region(logs, n)[:, c0:c1],
+                region(normed, n)[:, c0:c1],
+                ACT.Ln,
+                scale=log_scale[:, t : t + 1],
+                bias=is_zero[:, t : t + 1],
             )
 
         w2_b = keep.tile([P, N * PACK], BF16, name="w2_b", align_bytes=64)
@@ -277,13 +292,9 @@ def tile_picked_yhistf_ent_p_kernel(
         w2_s = keep.tile([P, N], U8, name="w2_s", align_bytes=64)
 
         def quantize_w2():
-            nc.gpsimd.tensor_scalar(
-                w2_b[:].rearrange("p (m j) -> p m j", j=PACK),
-                w2_raw[:].rearrange("p j m -> p m j"),
-                1.0,
-                0.0,
-                ALU.mult,
-                ALU.add,
+            nc.vector.tensor_copy(
+                out=w2_b[:].rearrange("p (c i j) -> p c j i", i=4, j=PACK),
+                in_=w2_raw[:].rearrange("p j (c i) -> p c j i", i=4),
             )
             nc.vector.quantize_mx(out=w2_q[:].bitcast(FP8X4), scales=w2_s[:], in_=w2_b[:])
 
@@ -291,14 +302,15 @@ def tile_picked_yhistf_ent_p_kernel(
 
         def weave(q):
             c0, c1 = PIECES[q]
-            planes = hid_planes[:].rearrange("p (t j) -> p t j", t=PACK)[:, :, c0:c1]
+
+            def walk(tile):
+                planes = tile[:].rearrange("p (t j) -> p t j", t=PACK)[:, :, c0:c1]
+                return planes.rearrange("p t (c i) -> p c t i", i=4)
+
             hid[q] = keep.tile([P, (c1 - c0) * PACK], BF16, name=f"hid{q}", align_bytes=64)
-            src = planes.rearrange("p t (c i) -> p c t i", i=4)
-            dst = hid[q][:].rearrange("p (c i t) -> p c t i", i=4, t=PACK)
-            if q in WEAVE_ON_SCALAR:
-                nc.scalar.copy(dst, src)
-            else:
-                nc.vector.tensor_copy(dst, src)
+            nc.vector.tensor_tensor(
+                hid[q][:].rearrange("p (c i t) -> p c t i", i=4, t=PACK), walk(normed), walk(logs), ALU.mult
+            )
 
         def poses(q):
             c0, c1 = PIECES[q]
@@ -306,7 +318,7 @@ def tile_picked_yhistf_ent_p_kernel(
             hid_q = keep.tile([P, width], U32, name=f"hid_q{q}", align_bytes=64)
             hid_s = keep.tile([P, width], U8, name=f"hid_s{q}", align_bytes=64)
             nc.vector.quantize_mx(out=hid_q[:].bitcast(FP8X4), scales=hid_s[:], in_=hid[q][:])
-            acc = psum.tile([P, HALF], F32, name="y")
+            acc = spare_bank(len(UNITS) - 1 + q)
             nc.tensor.matmul_mx(
                 out=acc[:, :width],
                 lhsT=w2_q[:].bitcast(FP8X4),
@@ -323,17 +335,16 @@ def tile_picked_yhistf_ent_p_kernel(
         for t in RESCALED:
             rescale(t)
         early = [u for u in UNITS if u + (1,) not in LATE_AFTER]
-        for t, h in sorted(early, key=lambda u: (u[0] // 2, u[1])):
+        for t, h in early:
             gather_beliefs(t, h)
+        gather_words(0, 0)
         cast_w1(0)
         gather_scales(0)
         quantize_w1(0)
         cast_w1(1)
-        gather_words(0, 0)
+        gather_words(0, 1)
         quantize_w1(1)
         gather_words(1, 0)
-        gather_scales(1)
-        gather_words(0, 1)
         predicted = []
 
         def predict_ready(done):
@@ -342,13 +353,15 @@ def tile_picked_yhistf_ent_p_kernel(
                     prediction(n)
                     predicted.append(n)
 
-        done = 0
+        done = -1
         predict_ready(done)
+        done = 0
         for step in range(len(UNITS) + 3):
             if step < len(UNITS):
                 likelihood(step)
             if step == 0:
                 gather_words(1, 1)
+                gather_scales(1)
             if step == 2:
                 unit_factors()
             if step == 4:
@@ -368,13 +381,14 @@ def tile_picked_yhistf_ent_p_kernel(
                 done = step - 2
             predict_ready(done)
         by_half = sorted(range(len(UNITS)), key=lambda n: UNITS[n][1])
-        for n in by_half:
+        for n in by_half[:-1]:
             logarithm(n)
+        for c0 in range(0, HALF, 256):
+            logarithm(by_half[-1], c0, c0 + 256)
         for h in range(HALVES):
-            for n in by_half[h * PACK : (h + 1) * PACK]:
-                hidden(n)
             mine = [q for q in range(len(PIECES)) if PIECES[q][0] // HALF == h]
             for q in mine:
                 weave(q)
-            for q in mine:
-                poses(q)
+                if q != mine[0]:
+                    poses(q - 1)
+            poses(mine[-1])

@@ -25,12 +25,17 @@ HALVES = S // HALF
 BLOCKS = HALF // P
 GROUPS = 2 * HALF // D
 UNITS = [(2 * a + b, h) for a in range(2) for h in range(HALVES) for b in range(2)]
-WORK_BANKS = 5
+SCALED_ON_VECTOR = ((1, 0, 0), (1, 0, 1))
+Y_BANK = (4, 5, 6, 7, 6, 7, 6, 7)
+WORK_BANK = (0, 1, 2, 3, 4, 5, 0, 1)
+OUT_BANK = (6, 7, 2, 3)
+BATCHES = ((0, 1, 2, 3), (4, 5), (6, 7))
+BATCH_OF = {n: (k, i) for k, batch in enumerate(BATCHES) for i, n in enumerate(batch)}
 CAST_ON_GPSIMD = ()
 VECTOR_GATHERS = ()
 RESCALED = sorted(set(t for t, h in VECTOR_GATHERS))
 TREE_ON_VECTOR = (0, 1, 2, 3)
-LATE_AFTER = {(3, 0, 0): 0, (3, 0, 1): 1, (2, 1, 0): 2, (2, 1, 1): 3, (3, 1, 0): 4, (3, 1, 1): 5}
+LATE_AFTER = {(2, 1): 3, (3, 1): 4}
 PIECES = ((0, 128), (128, 256), (256, 384), (384, 512), (512, 768), (768, 896), (896, 1024))
 WEAVE_ON_SCALAR = (0, 1)
 
@@ -47,7 +52,9 @@ def tile_picked_yhistf_ent_p_kernel(
         offs_t = keep.tile([P, S // 16], U16, name="offs_t")
         mv1_t = keep.tile([P, S // 16], U16, name="mv1_t")
         mv2_t = keep.tile([P, S // 16], U16, name="mv2_t")
-        bel_t = [keep.tile([P, S], F32, name=f"bel{t}") for t in range(PACK)]
+        first_two = keep.tile([P, 2 * S], F32, name="first_two")
+        bel_t = [first_two[:, S:], first_two[:, :S]]
+        bel_t = bel_t + [keep.tile([P, S], F32, name=f"bel{t}")[:] for t in range(2, PACK)]
         xw = [keep.tile([P, T], I32, name=f"xw{g}") for g in range(PASSES)]
         xs = keep.tile([P, T], U8, name="xs")
         w1_raw = [keep.tile([P, PACK, H], F32, name=f"w1_raw{g}") for g in range(PASSES)]
@@ -80,15 +87,15 @@ def tile_picked_yhistf_ent_p_kernel(
         load_beliefs(0)
         nc.sync.dma_start(mv1_t[:], mv1)
         nc.sync.dma_start(mv2_t[:], mv2)
+        load_beliefs(1)
         load_words(0)
         nc.sync.dma_start(offs_t[:], offs)
-        load_beliefs(1)
+        load_beliefs(2)
+        load_beliefs(3)
         load_scales()
         load_w1(0)
-        load_beliefs(2)
         load_w1(1)
         load_words(1)
-        load_beliefs(3)
         nc.sync.dma_start(out=unit_t[:], in_=unit.rearrange("(p t) o -> p (t o)", t=PACK))
         nc.sync.dma_start(out=w2_raw[:], in_=w2.rearrange("(p j) m -> p j m", j=PACK))
 
@@ -131,6 +138,7 @@ def tile_picked_yhistf_ent_p_kernel(
 
         moved = {}
         lik = {}
+        shared = {n: keep.tile([P, 2 * HALF], F32, name=f"shared{n}") for n in LATE_AFTER.values()}
 
         def lead_weight(t):
             return 0.3 if t in RESCALED else 0.5
@@ -143,13 +151,20 @@ def tile_picked_yhistf_ent_p_kernel(
 
         def gather_beliefs(t, h):
             for which, lst, weight in ((0, mv1_t, 0.3), (1, mv2_t, 0.2)):
-                if (t, h, which) in LATE_AFTER:
-                    moved[which, t, h] = lik[LATE_AFTER[t, h, which]]
+                if (t, h) in LATE_AFTER:
+                    moved[which, t, h] = shared[LATE_AFTER[t, h]][:, which * HALF : (which + 1) * HALF]
                 else:
-                    moved[which, t, h] = keep.tile([P, HALF], F32, name=f"moved_{which}{t}{h}")
+                    moved[which, t, h] = keep.tile([P, HALF], F32, name=f"moved_{which}{t}{h}")[:]
                 looked_up = bel_t[t][:].indirect(lst[:, cols(h)])
-                if which == 0 and (t, h) in VECTOR_GATHERS:
-                    nc.vector.tensor_copy(moved[which, t, h][:], looked_up)
+                if (t, h, which) in SCALED_ON_VECTOR:
+                    nc.vector.tensor_scalar(
+                        moved[which, t, h][:],
+                        first_two[:].indirect(lst[:, cols(h)]),
+                        weight / lead_weight(t),
+                        0.0,
+                        ALU.mult,
+                        ALU.add,
+                    )
                 else:
                     nc.scalar.activation(moved[which, t, h][:], looked_up, ACT.Copy, scale=weight / lead_weight(t))
 
@@ -159,15 +174,12 @@ def tile_picked_yhistf_ent_p_kernel(
 
         banks = [psum.tile([P, HALF], F32, name=f"bank{i}", bufs=1) for i in range(8)]
 
-        def spare_bank(i):
-            return banks[WORK_BANKS + i % (8 - WORK_BANKS)]
-
         work = {}
         sums = {}
 
         def likelihood(n):
             t, h = UNITS[n]
-            y = banks[WORK_BANKS - 1] if n == 0 else spare_bank(n - 1)
+            y = banks[Y_BANK[n]]
             for b in range(BLOCKS):
                 blk = slice(b * P, (b + 1) * P)
                 for g in range(PASSES):
@@ -181,14 +193,17 @@ def tile_picked_yhistf_ent_p_kernel(
                         stop=(g == PASSES - 1),
                     )
             nc.scalar.activation(scratch[:, n], y[:].rearrange("p (r c) -> p r c", r=len(UNITS)), ACT.Tanh)
-            lik[n] = keep.tile([P, HALF], F32, name=f"lik{n}")
+            if n in shared:
+                lik[n] = shared[n][:, HALF // 2 : HALF // 2 + HALF]
+            else:
+                lik[n] = keep.tile([P, HALF], F32, name=f"lik{n}")[:]
             nc.scalar.activation(
                 lik[n][:].rearrange("p (r c) -> p r c", r=len(UNITS)), scratch[:, n], ACT.Exp, scale=1.2
             )
 
         def prediction(n):
             t, h = UNITS[n]
-            work[n] = banks[n % WORK_BANKS]
+            work[n] = banks[WORK_BANK[n]]
             for b in range(BLOCKS):
                 blk = slice(b * P, (b + 1) * P)
                 terms = (
@@ -209,10 +224,11 @@ def tile_picked_yhistf_ent_p_kernel(
                 nc.tensor.transpose(work[n][:, blk], turned[:, blk], ident[:])
 
         def tile_sums(n):
-            if n % 2 == 0:
-                sums[n // 2] = ring.tile([P, GROUPS], F32, name="sums")
+            k, i = BATCH_OF[n]
+            if i == 0:
+                sums[k] = keep.tile([P, len(BATCHES[k]) * P], F32, name=f"sums{k}")
             nc.vector.tensor_reduce(
-                sums[n // 2][:, n % 2 * P : (n % 2 + 1) * P],
+                sums[k][:, i * P : (i + 1) * P],
                 work[n][:].rearrange("p (v d) -> p v d", d=D),
                 mybir.AxisListType.X,
                 ALU.add,
@@ -225,26 +241,27 @@ def tile_picked_yhistf_ent_p_kernel(
 
         def reciprocals(k):
             mul = nc.vector if k in TREE_ON_VECTOR else nc.gpsimd
-            den = ring.tile([P, GROUPS], F32, name="den")
-            mul.tensor_scalar(den[:], sums[k][:], 1.0, 0.2 / lead_weight(UNITS[2 * k][0]), ALU.mult, ALU.add)
-            pair = ring.tile([P, GROUPS // 2], F32, name="pair")
-            mul.tensor_tensor(pair[:], den[:, : GROUPS // 2], den[:, GROUPS // 2 :], ALU.mult)
-            quad = ring.tile([P, GROUPS // 4], F32, name="quad")
-            mul.tensor_tensor(quad[:], pair[:, : GROUPS // 4], pair[:, GROUPS // 4 :], ALU.mult)
-            quad_inv = ring.tile([P, GROUPS // 4], F32, name="quad_inv")
+            width = len(BATCHES[k]) * P
+            den = keep.tile([P, width], F32, name=f"den{k}")
+            mul.tensor_scalar(den[:], sums[k][:], 1.0, 0.2 / lead_weight(UNITS[BATCHES[k][0]][0]), ALU.mult, ALU.add)
+            pair = keep.tile([P, width // 2], F32, name=f"pair{k}")
+            mul.tensor_tensor(pair[:], den[:, : width // 2], den[:, width // 2 :], ALU.mult)
+            quad = keep.tile([P, width // 4], F32, name=f"quad{k}")
+            mul.tensor_tensor(quad[:], pair[:, : width // 4], pair[:, width // 4 :], ALU.mult)
+            quad_inv = keep.tile([P, width // 4], F32, name=f"quad_inv{k}")
             nc.vector.reciprocal(quad_inv[:], quad[:])
-            pair_inv = ring.tile([P, GROUPS // 2], F32, name="pair_inv")
+            pair_inv = keep.tile([P, width // 2], F32, name=f"pair_inv{k}")
             mul.tensor_tensor(
                 halves(pair_inv[:]),
                 halves(pair[:])[:, ::-1, :],
-                quad_inv[:].unsqueeze(1).to_broadcast([P, 2, GROUPS // 4]),
+                quad_inv[:].unsqueeze(1).to_broadcast([P, 2, width // 4]),
                 ALU.mult,
             )
-            inverse[k] = ring.tile([P, GROUPS], F32, name="inverse")
+            inverse[k] = keep.tile([P, width], F32, name=f"inverse{k}")
             mul.tensor_tensor(
                 halves(inverse[k][:]),
                 halves(den[:])[:, ::-1, :],
-                pair_inv[:].unsqueeze(1).to_broadcast([P, 2, GROUPS // 2]),
+                pair_inv[:].unsqueeze(1).to_broadcast([P, 2, width // 2]),
                 ALU.mult,
             )
 
@@ -268,11 +285,12 @@ def tile_picked_yhistf_ent_p_kernel(
 
         def normalise(n):
             t = UNITS[n][0]
+            k, i = BATCH_OF[n]
             nc.vector.scalar_tensor_tensor(
                 region(normed, n).rearrange("p (v d) -> p v d", d=D),
                 work[n][:].rearrange("p (v d) -> p v d", d=D),
                 half_unit[:, t : t + 1],
-                inverse[n // 2][:, n % 2 * P : (n % 2 + 1) * P].unsqueeze(2).to_broadcast([P, P, D]),
+                inverse[k][:, i * P : (i + 1) * P].unsqueeze(2).to_broadcast([P, P, D]),
                 ALU.mult,
                 ALU.mult,
             )
@@ -318,7 +336,7 @@ def tile_picked_yhistf_ent_p_kernel(
             hid_q = keep.tile([P, width], U32, name=f"hid_q{q}", align_bytes=64)
             hid_s = keep.tile([P, width], U8, name=f"hid_s{q}", align_bytes=64)
             nc.vector.quantize_mx(out=hid_q[:].bitcast(FP8X4), scales=hid_s[:], in_=hid[q][:])
-            acc = spare_bank(len(UNITS) - 1 + q)
+            acc = banks[OUT_BANK[q % len(OUT_BANK)]]
             nc.tensor.matmul_mx(
                 out=acc[:, :width],
                 lhsT=w2_q[:].bitcast(FP8X4),
@@ -334,7 +352,7 @@ def tile_picked_yhistf_ent_p_kernel(
 
         for t in RESCALED:
             rescale(t)
-        early = [u for u in UNITS if u + (1,) not in LATE_AFTER]
+        early = [u for u in UNITS if u not in LATE_AFTER]
         for t, h in early:
             gather_beliefs(t, h)
         gather_words(0, 0)
@@ -345,41 +363,32 @@ def tile_picked_yhistf_ent_p_kernel(
         gather_words(0, 1)
         quantize_w1(1)
         gather_words(1, 0)
-        predicted = []
+        for n in range(4):
+            prediction(n)
 
-        def predict_ready(done):
-            for n, (t, h) in enumerate(UNITS):
-                if n not in predicted and (1, t, h) in moved and n - WORK_BANKS < done and len(predicted) == n:
+        def likelihoods(upto):
+            for n in range(len(lik), min(upto, len(UNITS))):
+                likelihood(n)
+                if n == 0:
+                    gather_words(1, 1)
+                    gather_scales(1)
+                    unit_factors()
+                    quantize_w2()
+
+        for k, batch in enumerate(BATCHES):
+            for n in batch:
+                likelihoods(n + 3)
+                if n >= 4:
                     prediction(n)
-                    predicted.append(n)
-
-        done = -1
-        predict_ready(done)
-        done = 0
-        for step in range(len(UNITS) + 3):
-            if step < len(UNITS):
-                likelihood(step)
-            if step == 0:
-                gather_words(1, 1)
-                gather_scales(1)
-            if step == 2:
-                unit_factors()
-            if step == 4:
-                quantize_w2()
-            if 1 <= step <= len(UNITS):
-                posterior(step - 1)
-            for t, h in UNITS:
-                if LATE_AFTER.get((t, h, 1)) == step - 1:
-                    gather_beliefs(t, h)
-            if 2 <= step <= len(UNITS) + 1:
-                tile_sums(step - 2)
-                if step % 2 == 1:
-                    reciprocals((step - 2) // 2)
-            if step >= 4 and step % 2 == 0:
-                normalise(step - 4)
-                normalise(step - 3)
-                done = step - 2
-            predict_ready(done)
+                posterior(n)
+                for t, h in UNITS:
+                    if LATE_AFTER.get((t, h)) == n:
+                        gather_beliefs(t, h)
+            for n in batch:
+                tile_sums(n)
+            reciprocals(k)
+            for n in batch:
+                normalise(n)
         by_half = sorted(range(len(UNITS)), key=lambda n: UNITS[n][1])
         for n in by_half[:-1]:
             logarithm(n)

import math
from contextlib import ExitStack

import concourse.mybir as mybir
from concourse.masks import make_identity

K, T, S, D, N, H = 1024, 2048, 1024, 4, 128, 512
FLOPS = 2 * K * H * S + 2 * H * N * S

F32 = mybir.dt.float32
BF16 = mybir.dt.bfloat16
I32 = mybir.dt.int32
U32 = mybir.dt.uint32
U16 = mybir.dt.uint16
U8 = mybir.dt.uint8
FP8X4 = mybir.dt.float8_e4m3fn_x4
ALU = mybir.AluOpType
ACT = mybir.ActivationFunctionType

P = 128
PACK = 4
PASSES = K // (P * PACK)
HALF = 512
HALVES = S // HALF
BLOCKS = HALF // P
GROUPS = 2 * HALF // D
UNITS = [(2 * a + b, h) for a in range(2) for h in range(HALVES) for b in range(2)]
SCALED_ON_VECTOR = ((1, 0, 0), (1, 0, 1))
Y_BANK = (4, 5, 6, 7, 6, 7, 6, 7)
WORK_BANK = (0, 1, 2, 3, 4, 5, 0, 1)
OUT_BANK = (6, 7, 2, 3)
BATCHES = ((0, 1, 2, 3), (4, 5), (6, 7))
BATCH_OF = {n: (k, i) for k, batch in enumerate(BATCHES) for i, n in enumerate(batch)}
CAST_ON_GPSIMD = ()
VECTOR_GATHERS = ()
RESCALED = sorted(set(t for t, h in VECTOR_GATHERS))
TREE_ON_VECTOR = (0, 1, 2, 3)
LATE_AFTER = {(2, 1): 3, (3, 1): 4}
PIECES = ((0, 128), (128, 256), (256, 384), (384, 512), (512, 768), (768, 896), (896, 1024))
WEAVE_ON_SCALAR = (0, 1)


def tile_picked_yhistf_ent_p_kernel(
    tc, x_words, x_scales, w1, bel, unit, w2, offs, mv1, mv2, out
):
    nc = tc.nc
    with ExitStack() as ctx:
        keep = ctx.enter_context(tc.tile_pool(name="keep", bufs=1))
        ring = ctx.enter_context(tc.tile_pool(name="ring", bufs=2))
        psum = ctx.enter_context(tc.psum_pool(name="psum", bufs=2))

        offs_t = keep.tile([P, S // 16], U16, name="offs_t")
        mv1_t = keep.tile([P, S // 16], U16, name="mv1_t")
        mv2_t = keep.tile([P, S // 16], U16, name="mv2_t")
        first_two = keep.tile([P, 2 * S], F32, name="first_two")
        bel_t = [first_two[:, S:], first_two[:, :S]]
        bel_t = bel_t + [keep.tile([P, S], F32, name=f"bel{t}")[:] for t in range(2, PACK)]
        xw = [keep.tile([P, T], I32, name=f"xw{g}") for g in range(PASSES)]
        xs = keep.tile([P, T], U8, name="xs")
        w1_raw = [keep.tile([P, PACK, H], F32, name=f"w1_raw{g}") for g in range(PASSES)]
        w2_raw = keep.tile([P, PACK, N], F32, name="w2_raw")
        unit_t = keep.tile([P, PACK], F32, name="unit_t")
        ident = keep.tile([P, P], F32, name="ident")

        nc.gpsimd.memset(xs[:].bitcast(I32), 0)
        make_identity(nc, ident[:])

        bel_rows = bel.rearrange("(p t) j -> t p j", t=PACK)

        def load_beliefs(t):
            nc.sync.dma_start(out=bel_t[t][:], in_=bel_rows[t])

        def load_words(g):
            nc.sync.dma_start(out=xw[g][:], in_=x_words[g].rearrange("p c r -> p (c r)").bitcast(I32))

        def load_w1(g):
            rows = w1[g * P * PACK : (g + 1) * P * PACK, :]
            nc.sync.dma_start(out=w1_raw[g][:], in_=rows.rearrange("(p j) c -> p j c", j=PACK))

        def load_scales():
            for q in range(4):
                nc.sync.dma_start(
                    out=xs[32 * q : 32 * q + 4 * PASSES, :].bitcast(I32),
                    in_=x_scales[:, 4 * q : 4 * q + 4, :].bitcast(I32),
                )

        load_beliefs(0)
        nc.sync.dma_start(mv1_t[:], mv1)
        nc.sync.dma_start(mv2_t[:], mv2)
        load_beliefs(1)
        load_words(0)
        nc.sync.dma_start(offs_t[:], offs)
        load_beliefs(2)
        load_beliefs(3)
        load_scales()
        load_w1(0)
        load_w1(1)
        load_words(1)
        nc.sync.dma_start(out=unit_t[:], in_=unit.rearrange("(p t) o -> p (t o)", t=PACK))
        nc.sync.dma_start(out=w2_raw[:], in_=w2.rearrange("(p j) m -> p j m", j=PACK))

        def cols(h):
            return slice(h * HALF // 16, (h + 1) * HALF // 16)

        gw = {}
        gs = {}

        def gather_words(g, h):
            gw[g, h] = keep.tile([P, HALF], U32, name=f"gw{g}{h}", align_bytes=64)
            nc.vector.tensor_copy(gw[g, h][:], xw[g][:].bitcast(U32).indirect(offs_t[:, cols(h)]))

        def gather_scales(h):
            gs[h] = keep.tile([P, HALF], U8, name=f"gs{h}", align_bytes=64)
            nc.vector.tensor_copy(gs[h][:], xs[:].indirect(offs_t[:, cols(h)]))

        w1_q = [keep.tile([P, H], U32, name=f"w1_q{g}", align_bytes=64) for g in range(PASSES)]
        w1_s = [keep.tile([P, H], U8, name=f"w1_s{g}", align_bytes=64) for g in range(PASSES)]
        w1_b = [keep.tile([P, H * PACK], BF16, name=f"w1_b{g}", align_bytes=64) for g in range(PASSES)]

        def cast_w1(g):
            if g in CAST_ON_GPSIMD:
                nc.gpsimd.tensor_scalar(
                    w1_b[g][:].rearrange("p (t m j) -> p t m j", t=PACK, j=PACK),
                    w1_raw[g][:].rearrange("p j (m t) -> p t m j", t=PACK),
                    1.0,
                    0.0,
                    ALU.mult,
                    ALU.add,
                )
            else:
                nc.vector.tensor_copy(
                    out=w1_b[g][:].rearrange("p (t m j) -> p m j t", t=PACK, j=PACK),
                    in_=w1_raw[g][:].rearrange("p j (m t) -> p m j t", t=PACK),
                )

        def quantize_w1(g):
            nc.vector.quantize_mx(out=w1_q[g][:].bitcast(FP8X4), scales=w1_s[g][:], in_=w1_b[g][:])

        moved = {}
        lik = {}
        shared = {n: keep.tile([P, 2 * HALF], F32, name=f"shared{n}") for n in LATE_AFTER.values()}

        def lead_weight(t):
            return 0.3 if t in RESCALED else 0.5

        stay = {t: bel_t[t] for t in range(PACK)}

        def rescale(t):
            stay[t] = keep.tile([P, S], F32, name=f"stay{t}")
            nc.gpsimd.tensor_scalar(stay[t][:], bel_t[t][:], 0.5 / 0.3, 0.0, ALU.mult, ALU.add)

        def gather_beliefs(t, h):
            for which, lst, weight in ((0, mv1_t, 0.3), (1, mv2_t, 0.2)):
                if (t, h) in LATE_AFTER:
                    moved[which, t, h] = shared[LATE_AFTER[t, h]][:, which * HALF : (which + 1) * HALF]
                else:
                    moved[which, t, h] = keep.tile([P, HALF], F32, name=f"moved_{which}{t}{h}")[:]
                looked_up = bel_t[t][:].indirect(lst[:, cols(h)])
                if (t, h, which) in SCALED_ON_VECTOR:
                    nc.vector.tensor_scalar(
                        moved[which, t, h][:],
                        first_two[:].indirect(lst[:, cols(h)]),
                        weight / lead_weight(t),
                        0.0,
                        ALU.mult,
                        ALU.add,
                    )
                else:
                    nc.scalar.activation(moved[which, t, h][:], looked_up, ACT.Copy, scale=weight / lead_weight(t))

        logs = keep.tile([P, PACK * S], F32, name="logs")
        normed = keep.tile([P, PACK * S], F32, name="normed")
        scratch = logs[:].rearrange("p (r n c) -> p n r c", r=len(UNITS), n=len(UNITS))

        banks = [psum.tile([P, HALF], F32, name=f"bank{i}", bufs=1) for i in range(8)]

        work = {}
        sums = {}

        def likelihood(n):
            t, h = UNITS[n]
            y = banks[Y_BANK[n]]
            for b in range(BLOCKS):
                blk = slice(b * P, (b + 1) * P)
                for g in range(PASSES):
                    nc.tensor.matmul_mx(
                        out=y[:, blk],
                        lhsT=gw[g, h][:, blk].bitcast(FP8X4),
                        lhsT_scale=gs[h][4 * g :, blk],
                        rhs=w1_q[g][:, t * P : (t + 1) * P].bitcast(FP8X4),
                        rhs_scale=w1_s[g][:, t * P : (t + 1) * P],
                        start=(g == 0),
                        stop=(g == PASSES - 1),
                    )
            nc.scalar.activation(scratch[:, n], y[:].rearrange("p (r c) -> p r c", r=len(UNITS)), ACT.Tanh)
            if n in shared:
                lik[n] = shared[n][:, HALF // 2 : HALF // 2 + HALF]
            else:
                lik[n] = keep.tile([P, HALF], F32, name=f"lik{n}")[:]
            nc.scalar.activation(
                lik[n][:].rearrange("p (r c) -> p r c", r=len(UNITS)), scratch[:, n], ACT.Exp, scale=1.2
            )

        def prediction(n):
            t, h = UNITS[n]
            work[n] = banks[WORK_BANK[n]]
            for b in range(BLOCKS):
                blk = slice(b * P, (b + 1) * P)
                terms = (
                    stay[t][:, h * HALF + b * P : h * HALF + (b + 1) * P],
                    moved[0, t, h][:, blk],
                    moved[1, t, h][:, blk],
                )
                for i, term in enumerate(terms):
                    nc.tensor.matmul(
                        work[n][:, blk], term, ident[:], start=(i == 0), stop=(i == len(terms) - 1), is_transpose=True
                    )

        def posterior(n):
            turned = ring.tile([P, HALF], F32, name="turned")
            nc.vector.tensor_tensor(turned[:], work[n][:], lik[n][:], ALU.mult)
            for b in range(BLOCKS):
                blk = slice(b * P, (b + 1) * P)
                nc.tensor.transpose(work[n][:, blk], turned[:, blk], ident[:])

        def tile_sums(n):
            k, i = BATCH_OF[n]
            if i == 0:
                sums[k] = keep.tile([P, len(BATCHES[k]) * P], F32, name=f"sums{k}")
            nc.vector.tensor_reduce(
                sums[k][:, i * P : (i + 1) * P],
                work[n][:].rearrange("p (v d) -> p v d", d=D),
                mybir.AxisListType.X,
                ALU.add,
            )

        inverse = {}

        def halves(ap):
            return ap.rearrange("p (a n) -> p a n", a=2)

        def reciprocals(k):
            mul = nc.vector if k in TREE_ON_VECTOR else nc.gpsimd
            width = len(BATCHES[k]) * P
            den = keep.tile([P, width], F32, name=f"den{k}")
            mul.tensor_scalar(den[:], sums[k][:], 1.0, 0.2 / lead_weight(UNITS[BATCHES[k][0]][0]), ALU.mult, ALU.add)
            pair = keep.tile([P, width // 2], F32, name=f"pair{k}")
            mul.tensor_tensor(pair[:], den[:, : width // 2], den[:, width // 2 :], ALU.mult)
            quad = keep.tile([P, width // 4], F32, name=f"quad{k}")
            mul.tensor_tensor(quad[:], pair[:, : width // 4], pair[:, width // 4 :], ALU.mult)
            quad_inv = keep.tile([P, width // 4], F32, name=f"quad_inv{k}")
            nc.vector.reciprocal(quad_inv[:], quad[:])
            pair_inv = keep.tile([P, width // 2], F32, name=f"pair_inv{k}")
            mul.tensor_tensor(
                halves(pair_inv[:]),
                halves(pair[:])[:, ::-1, :],
                quad_inv[:].unsqueeze(1).to_broadcast([P, 2, width // 4]),
                ALU.mult,
            )
            inverse[k] = keep.tile([P, width], F32, name=f"inverse{k}")
            mul.tensor_tensor(
                halves(inverse[k][:]),
                halves(den[:])[:, ::-1, :],
                pair_inv[:].unsqueeze(1).to_broadcast([P, 2, width // 2]),
                ALU.mult,
            )

        half_unit = keep.tile([P, PACK], F32, name="half_unit")

        is_zero = keep.tile([P, PACK], F32, name="is_zero")
        safe = keep.tile([P, PACK], F32, name="safe")
        safe_inv = keep.tile([P, PACK], F32, name="safe_inv")
        log_scale = keep.tile([P, PACK], F32, name="log_scale")

        def unit_factors():
            nc.vector.tensor_scalar_mul(half_unit[:], unit_t[:], 0.5)
            nc.vector.tensor_single_scalar(is_zero[:], unit_t[:], 0.0, ALU.is_equal)
            nc.vector.tensor_tensor(safe[:], unit_t[:], is_zero[:], ALU.add)
            nc.vector.reciprocal(safe_inv[:], safe[:])
            nc.vector.tensor_scalar_mul(log_scale[:], safe_inv[:], 2.0 * math.exp(2.0))

        def region(tile, n):
            t, h = UNITS[n]
            return tile[:, t * S + h * HALF : t * S + (h + 1) * HALF]

        def normalise(n):
            t = UNITS[n][0]
            k, i = BATCH_OF[n]
            nc.vector.scalar_tensor_tensor(
                region(normed, n).rearrange("p (v d) -> p v d", d=D),
                work[n][:].rearrange("p (v d) -> p v d", d=D),
                half_unit[:, t : t + 1],
                inverse[k][:, i * P : (i + 1) * P].unsqueeze(2).to_broadcast([P, P, D]),
                ALU.mult,
                ALU.mult,
            )

        def logarithm(n, c0=0, c1=HALF):
            t = UNITS[n][0]
            nc.scalar.activation(
                region(logs, n)[:, c0:c1],
                region(normed, n)[:, c0:c1],
                ACT.Ln,
                scale=log_scale[:, t : t + 1],
                bias=is_zero[:, t : t + 1],
            )

        w2_b = keep.tile([P, N * PACK], BF16, name="w2_b", align_bytes=64)
        w2_q = keep.tile([P, N], U32, name="w2_q", align_bytes=64)
        w2_s = keep.tile([P, N], U8, name="w2_s", align_bytes=64)

        def quantize_w2():
            nc.vector.tensor_copy(
                out=w2_b[:].rearrange("p (c i j) -> p c j i", i=4, j=PACK),
                in_=w2_raw[:].rearrange("p j (c i) -> p c j i", i=4),
            )
            nc.vector.quantize_mx(out=w2_q[:].bitcast(FP8X4), scales=w2_s[:], in_=w2_b[:])

        hid = {}

        def weave(q):
            c0, c1 = PIECES[q]

            def walk(tile):
                planes = tile[:].rearrange("p (t j) -> p t j", t=PACK)[:, :, c0:c1]
                return planes.rearrange("p t (c i) -> p c t i", i=4)

            hid[q] = keep.tile([P, (c1 - c0) * PACK], BF16, name=f"hid{q}", align_bytes=64)
            nc.vector.tensor_tensor(
                hid[q][:].rearrange("p (c i t) -> p c t i", i=4, t=PACK), walk(normed), walk(logs), ALU.mult
            )

        def poses(q):
            c0, c1 = PIECES[q]
            width = c1 - c0
            hid_q = keep.tile([P, width], U32, name=f"hid_q{q}", align_bytes=64)
            hid_s = keep.tile([P, width], U8, name=f"hid_s{q}", align_bytes=64)
            nc.vector.quantize_mx(out=hid_q[:].bitcast(FP8X4), scales=hid_s[:], in_=hid[q][:])
            acc = banks[OUT_BANK[q % len(OUT_BANK)]]
            nc.tensor.matmul_mx(
                out=acc[:, :width],
                lhsT=w2_q[:].bitcast(FP8X4),
                lhsT_scale=w2_s[:],
                rhs=hid_q[:].bitcast(FP8X4),
                rhs_scale=hid_s[:],
                start=True,
                stop=True,
            )
            result = keep.tile([P, width], F32, name=f"result{q}")
            nc.scalar.copy(result[:], acc[:, :width])
            nc.sync.dma_start(out=out[:, c0:c1], in_=result[:])

        for t in RESCALED:
            rescale(t)
        early = [u for u in UNITS if u not in LATE_AFTER]
        for t, h in early:
            gather_beliefs(t, h)
        gather_words(0, 0)
        cast_w1(0)
        gather_scales(0)
        quantize_w1(0)
        cast_w1(1)
        gather_words(0, 1)
        quantize_w1(1)
        gather_words(1, 0)
        for n in range(4):
            prediction(n)

        def likelihoods(upto):
            for n in range(len(lik), min(upto, len(UNITS))):
                likelihood(n)
                if n == 0:
                    gather_words(1, 1)
                    gather_scales(1)
                    unit_factors()
                    quantize_w2()

        for k, batch in enumerate(BATCHES):
            for n in batch:
                likelihoods(n + 3)
                if n >= 4:
                    prediction(n)
                posterior(n)
                for t, h in UNITS:
                    if LATE_AFTER.get((t, h)) == n:
                        gather_beliefs(t, h)
            for n in batch:
                tile_sums(n)
            reciprocals(k)
            for n in batch:
                normalise(n)
        by_half = sorted(range(len(UNITS)), key=lambda n: UNITS[n][1])
        for n in by_half[:-1]:
            logarithm(n)
        for c0 in range(0, HALF, 256):
            logarithm(by_half[-1], c0, c0 + 256)
        for h in range(HALVES):
            mine = [q for q in range(len(PIECES)) if PIECES[q][0] // HALF == h]
            for q in mine:
                weave(q)
                if q != mine[0]:
                    poses(q - 1)
            poses(mine[-1])
